import numpy as np, ml_dtypes
CORES = [19,147,275,403]
N = 4
TOK, CAP, FF = 256, 80, 8
def entries(a): return a.T.reshape(-1)
def pack(v, P): return np.ascontiguousarray(np.asarray(v, np.int32).reshape(-1, P).T)
def lists(rng, how):
    E = rng.integers(0, N, (N, TOK))
    if how == "hot": E[:] = rng.integers(N)
    if how == "none": E = (int(rng.integers(N)) + 1 + rng.integers(0, N - 1, (N, TOK))) % N
    if how == "skew": E = np.where(rng.random((N, TOK)) < 0.7, rng.integers(0, N, (N, 1)), E)
    if how == "even": E = np.stack([rng.permutation(np.arange(TOK) % N) for r in range(N)])
    if how == "own": E = np.repeat(np.arange(N).reshape(N, 1), TOK, axis=1)
    return {"ex": np.stack([pack(E[r], 16) for r in range(N)])}
def setup_inputs(rng):
    return dict({"x": rng.standard_normal((N, 128, TOK), dtype=np.float32).astype(ml_dtypes.bfloat16), "w1": (rng.standard_normal((N, 128, FF * 128), dtype=np.float32) / 8).astype(ml_dtypes.bfloat16), "w2": (rng.standard_normal((N, 128, FF * 128), dtype=np.float32) / 16).astype(ml_dtypes.bfloat16)}, **lists(rng, "uniform"))
def setup_inputs_even(rng):
    d = setup_inputs(rng); d.update(lists(rng, "even"))
    for k in ("x",): d[k] = (d[k].astype(np.float32) * 1024.0).astype(d[k].dtype)
    return d
def setup_inputs_hot(rng):
    d = setup_inputs(rng); d.update(lists(rng, "hot"))
    for k in ("x",): d[k] = (d[k].astype(np.float32) * (1 / 1024.0)).astype(d[k].dtype)
    return d
def setup_inputs_none(rng):
    d = setup_inputs(rng); d.update(lists(rng, "none"))
    return d
def setup_inputs_own(rng):
    d = setup_inputs(rng); d.update(lists(rng, "own"))
    return d
def setup_inputs_skew(rng):
    d = setup_inputs(rng); d.update(lists(rng, "skew"))
    return d
def check_inputs(x):
    bad = []
    if x["ex"].min() < 0 or x["ex"].max() >= N: bad.append("ex out of range")
    return bad
def reference(x, w1, w2, ex):
    X, W1, W2 = x.astype(np.float64), w1.astype(np.float64), w2.astype(np.float64)
    y = np.zeros((N, 128, TOK))
    for r in range(N):
        E = entries(ex[r]); place = np.array([np.sum(E[:t] == E[t]) for t in range(TOK)])
        for k in range(N):
            m = (E == k) & (place < CAP)
            y[r][:, m] = sum(W2[k][:, 128 * f:128 * f + 128].T @ np.maximum(W1[k][:, 128 * f:128 * f + 128].T @ X[r][:, m], 0.0) for f in range(FF))
    return {"y": y.astype(ml_dtypes.bfloat16)}

@@ -1,0 +1,205 @@
+from concourse.mybir import AluOpType, ActivationFunctionType
+
+CAP = 80
+SCRATCH = {
+    "ex4": ("sbuf", [64, 16], "int32"),
+    "kcol": ("sbuf", [64, 1], "float32"),
+    "b0col": ("sbuf", [64, 1], "float32"),
+    "shcol": ("sbuf", [64, 1], "float32"),
+    "sg": ("sbuf", [64, 64], "bfloat16"),
+    "la": ("sbuf", [64, 64], "bfloat16"),
+    "lb": ("sbuf", [64, 64], "bfloat16"),
+    "ri": ("sbuf", [64, 128], "int32"),
+    "ri2": ("sbuf", [64, 128], "int32"),
+    "r1": ("sbuf", [64, 128], "bfloat16"),
+    "rb": ("sbuf", [64, 128], "bfloat16"),
+    "m4z": ("sbuf", [64, 17], "bfloat16"),
+    "z16": ("sbuf", [64, 16], "float32"),
+    "offk": ("sbuf", [64, 16], "float32"),
+    "prod": ("sbuf", [64, 16], "bfloat16"),
+    "off": ("sbuf", [128, 16], "uint16"),
+    "off2": ("sbuf", [128, 16], "uint16"),
+    "xs": ("sbuf", [128, 256], "bfloat16"),
+    "sw": ("sbuf", [128, 512], "bfloat16"),
+    "xin": ("sbuf", [128, 320], "bfloat16"),
+    "w1s": ("sbuf", [128, 1024], "bfloat16"),
+    "w2s": ("sbuf", [128, 1024], "bfloat16"),
+    "hs": ("sbuf", [128, 2560], "bfloat16"),
+    "outb": ("sbuf", [128, 240], "bfloat16"),
+    "res": ("sbuf", [128, 1104], "bfloat16"),
+    "ys": ("sbuf", [128, 256], "bfloat16"),
+    "hp0": ("psum", [128, 512], "float32"),
+    "hp1": ("psum", [128, 512], "float32"),
+    "hp2": ("psum", [128, 512], "float32"),
+    "hp3": ("psum", [128, 512], "float32"),
+    "yp0": ("psum", [128, 512], "float32"),
+    "yp1": ("psum", [128, 512], "float32"),
+    "yp2": ("psum", [128, 512], "float32"),
+    "yp3": ("psum", [128, 512], "float32"),
+}
+SEMAPHORES = ["sex", "sx", "sw1", "sw2", "sy", "v", "gq", "pi1", "pi2", "pi3",
+              "mh0", "mh1", "mh2", "mh3", "rh0", "rh1", "rh2", "rh3",
+              "my0", "my1", "my2", "my3", "yc0", "yc1", "yc2", "yc3",
+              "aX", "aY", "aD", "rX", "rY", "rD", "ls", "gv", "ga"]
+
+
+def rank_program(g, core, T, topo):
+    rank = T.rank_of(core)
+    if rank is None:
+        return
+    A = AluOpType
+    V, S, P, Q = g.vector, g.scalar, g.tensor, g.sync
+    others = [c for c in T.cores if c != core]
+    X = [c for c in others if topo.same_plane(core, c)][0]
+    D = [c for c in others if not topo.may_write(core, c)][0]
+    Y = [c for c in others if c != X and c != D][0]
+    kap = [T.rank_of(Y), T.rank_of(X), T.rank_of(D), rank]
+
+    def engines(src, dst):
+        return bin(topo.mask(src, dst)).count("1")
+
+    tot = {}
+
+    def inc(ins, name, n=1):
+        ins.then_inc(T.sem[name], n)
+        tot[name] = tot.get(name, 0) + n
+        return tot[name]
+
+    def chain(queue, name, make):
+        if tot.get(name, 0):
+            queue.wait_ge(T.sem[name], tot[name])
+        return inc(make(), name)
+
+    def vop(make):
+        return chain(V, "v", make)
+
+    def gop(make):
+        return chain(g, "gq", make)
+
+    for k in range(4):
+        inc((Q if k < 2 else S).dma_start(T.ex4[16 * k:16 * k + 16, :], T.ex[:, :]), "sex", 16)
+    inc(Q.dma_start(T.xs[0:64, :], T.x[0:64, :]), "sx", 16)
+    inc(S.dma_start(T.xs[64:128, :], T.x[64:128, :]), "sx", 16)
+    inc(Q.dma_start(T.w1s[:, :], T.w1[:, :]), "sw1", 16)
+    inc(S.dma_start(T.w2s[:, :], T.w2[:, :]), "sw2", 16)
+
+    gop(lambda: g.iota(T.ri[:, :], [[1, 128]], 64, -1))
+    g_iota = tot["gq"]
+    vop(lambda: V.memset(T.sg[:, :], 1.0))
+    vop(lambda: V.memset(T.sg[:, 16:32], -1.0))
+    v_sg = vop(lambda: V.memset(T.sg[:, 48:64], -1.0))
+    g.wait_ge(T.sem.v, v_sg)
+    gop(lambda: g.affine_select(T.la[:, :], T.sg[:, :], [[1, 64]], A.is_gt, 0.0, 0, -1))
+    gop(lambda: g.affine_select(T.la[:, :], T.la[:, :], [[-16, 4], [0, 16]], A.is_ge, 0.0, 0, 1))
+    gop(lambda: g.affine_select(T.lb[:, :], T.sg[:, :], [[-1, 64]], A.is_ge, 0.0, 0, 1))
+    g_l = gop(lambda: g.affine_select(T.lb[:, :], T.lb[:, :], [[16, 4], [0, 16]], A.is_ge, 0.0, 15, -1))
+    for n, val in ((64, kap[3]), (48, kap[2]), (32, kap[1]), (16, kap[0])):
+        vop(lambda n=n, val=val: V.memset(T.kcol[0:n, :], float(val)))
+    vop(lambda: V.memset(T.m4z[:, 0:1], 0.0))
+    vop(lambda: V.memset(T.z16[:, :], 0.0))
+    for n, val in ((64, 255.0), (48, 0.0), (32, -1.0), (16, -256.0)):
+        vop(lambda n=n, val=val: V.memset(T.b0col[0:n, :], val))
+    vop(lambda: V.memset(T.sw[:, :], 0.0))
+    V.wait_ge(T.sem.gq, g_iota)
+    vop(lambda: V.tensor_scalar(T.ri2[:, :], T.ri[:, :], 15, None, A.bitwise_and))
+    vop(lambda: V.tensor_scalar(T.r1[:, :], T.ri2[:, :], 0, None, A.is_equal))
+
+    V.wait_ge(T.sem.sex, tot["sex"])
+    v_m4 = vop(lambda: V.tensor_scalar(T.m4z[:, 1:17], T.ex4[:, :], T.kcol[:, 0:1], None, A.is_equal))
+    P.wait_ge(T.sem.v, v_m4)
+    P.wait_ge(T.sem.gq, g_l)
+    inc(P.matmul(T.yp2[0:64, 0:16], T.la[:, :], T.m4z[:, 1:17], True, False), "pi1")
+    inc(P.matmul(T.yp2[0:64, 0:16], T.lb[:, :], T.m4z[:, 0:16], False, True), "pi1")
+    V.wait_ge(T.sem.pi1, tot["pi1"])
+    vop(lambda: V.tensor_tensor_scan(T.offk[:, :], T.yp2[0:64, 0:16], T.z16[:, :], T.b0col[:, 0:1], A.add, A.add))
+    v_prod = vop(lambda: V.tensor_tensor(T.prod[:, :], T.offk[:, :], T.m4z[:, 1:17], A.mult))
+    P.wait_ge(T.sem.v, v_prod)
+    inc(P.matmul(T.yp3[:, 0:16], T.r1[:, :], T.prod[:, :], True, True), "pi2")
+    V.wait_ge(T.sem.pi2, tot["pi2"])
+    vop(lambda: V.tensor_scalar(T.off[:, :], T.yp3[:, 0:16], 256.0, None, A.add))
+    V.wait_ge(T.sem.sx, tot["sx"])
+    v_sc = vop(lambda: V.tensor_copy(T.sw[:, 0:512].indirect(T.off[:, 0:16]), T.xs[:, :]))
+    for n, val in ((64, 512.0), (48, 256.0), (16, 0.0)):
+        vop(lambda n=n, val=val: V.memset(T.shcol[0:n, :], val))
+    v_rb = vop(lambda: V.tensor_scalar(T.rb[:, :], T.ri2[:, :], 0, T.shcol[:, 0:1], A.is_equal, A.mult))
+    vop(lambda: V.memset(T.res[:, 160:512], 0.0))
+    vop(lambda: V.memset(T.res[:, 672:1024], 0.0))
+
+    def send(dst, out_ap, in_ap, sem):
+        rid, pid = topo.addr(dst, core)
+        g.remote_dma(out_ap, in_ap, T.sem[sem], T.sem.ls, pid, rid, topo.mask(core, dst))
+        tot["ls"] = tot.get("ls", 0) + engines(core, dst)
+
+    for name, src in (("aX", X), ("aY", Y), ("aD", Y), ("rX", X), ("rY", Y), ("rD", X)):
+        tot[name] = engines(src, core)
+
+    g.wait_ge(T.sem.v, v_sc)
+    send(X, T.xin[:, 0:160], T.sw[:, 176:336], "aX")
+    send(Y, T.xin[:, 160:240], T.sw[:, 0:80], "aY")
+    g.wait_ge(T.sem.aX, tot["aX"])
+    send(Y, T.xin[:, 240:320], T.xin[:, 80:160], "aD")
+
+    hp = [T.hp0, T.hp1, T.hp2, T.hp3]
+    yp = [T.yp0, T.yp1, T.yp2, T.yp3]
+    blocks = [(T.sw[:, 432:512], None, T.res[:, 1024:1104]),
+              (T.xin[:, 0:80], "aX", T.outb[:, 160:240]),
+              (T.xin[:, 160:240], "aY", T.outb[:, 80:160]),
+              (T.xin[:, 240:320], "aD", T.outb[:, 0:80])]
+    P.wait_ge(T.sem.v, v_sc)
+    P.wait_ge(T.sem.sw1, tot["sw1"])
+    for b, (rhs, arr, dest) in enumerate(blocks):
+        if arr:
+            P.wait_ge(T.sem[arr], tot[arr])
+        for i in range(4):
+            if b:
+                P.wait_ge(T.sem["rh%d" % i], b)
+            for f in (2 * i, 2 * i + 1):
+                c = (f % 2) * CAP
+                inc(P.matmul(hp[i][:, c:c + CAP], T.w1s[:, 128 * f:128 * f + 128], rhs, True, True), "mh%d" % i)
+        for i in range(4):
+            h = T.hs[:, b * 640 + i * 160:b * 640 + i * 160 + 160]
+            E = V if i % 2 == 0 else S
+            E.wait_ge(T.sem["mh%d" % i], tot["mh%d" % i])
+            if i % 2 == 0:
+                inc(V.tensor_scalar(h, hp[i][:, 0:160], 0.0, None, A.max), "rh%d" % i)
+            else:
+                inc(S.activation(h, hp[i][:, 0:160], ActivationFunctionType.Relu), "rh%d" % i)
+        if b == 0:
+            P.wait_ge(T.sem.sw2, tot["sw2"])
+        for i in range(4):
+            P.wait_ge(T.sem["rh%d" % i], b + 1)
+            for f in (2 * i, 2 * i + 1):
+                c = b * 640 + f * CAP
+                inc(P.matmul(yp[b][:, 0:CAP], T.w2s[:, 128 * f:128 * f + 128], T.hs[:, c:c + CAP], f == 0, f == 7),
+                    "my%d" % b)
+        V.wait_ge(T.sem["my%d" % b], tot["my%d" % b])
+        inc(V.tensor_copy(dest, yp[b][:, 0:CAP]), "yc%d" % b)
+        if b == 0:
+            P.wait_ge(T.sem.yc0, tot["yc0"])
+            P.wait_ge(T.sem.v, v_rb)
+            inc(P.matmul(T.yp0[:, 0:16], T.r1[:, :], T.prod[:, :], True, False), "pi3")
+            inc(P.matmul(T.yp0[:, 0:16], T.rb[:, :], T.m4z[:, 1:17], False, True), "pi3")
+            V.wait_ge(T.sem.pi3, tot["pi3"])
+            vop(lambda: V.tensor_scalar(T.off2[:, :], T.yp0[:, 0:16], 256.0, None, A.add))
+
+    g.wait_ge(T.sem.yc1, tot["yc1"])
+    send(X, T.res[:, 512:592], T.outb[:, 160:240], "rX")
+    g.wait_ge(T.sem.yc2, tot["yc2"])
+    g.wait_ge(T.sem.yc3, tot["yc3"])
+    send(Y, T.res[:, 0:160], T.outb[:, 0:160], "rY")
+    g.wait_ge(T.sem.rY, tot["rY"])
+    send(X, T.res[:, 592:672], T.res[:, 0:80], "rD")
+
+    for E in (V, S):
+        E.wait_ge(T.sem.v, tot["v"])
+        for name in ("yc0", "rX", "rY", "rD"):
+            E.wait_ge(T.sem[name], tot[name])
+    inc(V.tensor_copy(T.ys[:, 0:128], T.res[:, 80:1104].indirect(T.off2[:, 0:8])), "gv")
+    inc(S.activation(T.ys[:, 128:256], T.res[:, 80:1104].indirect(T.off2[:, 8:16]), ActivationFunctionType.Copy), "ga")
+    Q.wait_ge(T.sem.gv, tot["gv"])
+    Q.wait_ge(T.sem.ga, tot["ga"])
+    inc(Q.dma_start(T.y[:, :], T.ys[:, :]), "sy", 16)
+
+    for name in SEMAPHORES:
+        if tot.get(name, 0):
+            g.wait_ge(T.sem[name], tot[name])

@@ -40,7 +40,7 @@ SCRATCH = {
 SEMAPHORES = ["sex", "sx", "sw1", "sw2", "sy", "v", "gq", "pi1", "pi2", "pi3",
               "mh0", "mh1", "mh2", "mh3", "rh0", "rh1", "rh2", "rh3",
               "my0", "my1", "my2", "my3", "yc0", "yc1", "yc2", "yc3",
-              "aX", "aY", "aD", "rX", "rY", "rD", "ls", "gv", "ga"]
+              "aP", "aX", "aY", "aD", "rP", "rX", "rY", "rD", "ls", "gv", "ga"]
 
 
 def rank_program(g, core, T, topo):
@@ -130,21 +130,22 @@ def rank_program(g, core, T, topo):
         g.remote_dma(out_ap, in_ap, T.sem[sem], T.sem.ls, pid, rid, topo.mask(core, dst))
         tot["ls"] = tot.get("ls", 0) + engines(core, dst)
 
-    for name, src in (("aX", X), ("aY", Y), ("aD", Y), ("rX", X), ("rY", Y), ("rD", X)):
+    for name, src in (("aP", X), ("aX", X), ("aY", Y), ("aD", Y), ("rP", X), ("rX", X), ("rY", Y), ("rD", Y)):
         tot[name] = engines(src, core)
 
     g.wait_ge(T.sem.v, v_sc)
-    send(X, T.xin[:, 0:160], T.sw[:, 176:336], "aX")
+    send(X, T.xin[:, 80:160], T.sw[:, 256:336], "aP")
     send(Y, T.xin[:, 160:240], T.sw[:, 0:80], "aY")
-    g.wait_ge(T.sem.aX, tot["aX"])
+    send(X, T.xin[:, 0:80], T.sw[:, 176:256], "aX")
+    g.wait_ge(T.sem.aP, tot["aP"])
     send(Y, T.xin[:, 240:320], T.xin[:, 80:160], "aD")
 
     hp = [T.hp0, T.hp1, T.hp2, T.hp3]
     yp = [T.yp0, T.yp1, T.yp2, T.yp3]
     blocks = [(T.sw[:, 432:512], None, T.res[:, 1024:1104]),
-              (T.xin[:, 0:80], "aX", T.outb[:, 160:240]),
               (T.xin[:, 160:240], "aY", T.outb[:, 80:160]),
-              (T.xin[:, 240:320], "aD", T.outb[:, 0:80])]
+              (T.xin[:, 240:320], "aD", T.outb[:, 0:80]),
+              (T.xin[:, 0:80], "aX", T.outb[:, 160:240])]
     P.wait_ge(T.sem.v, v_sc)
     P.wait_ge(T.sem.sw1, tot["sw1"])
     for b, (rhs, arr, dest) in enumerate(blocks):
@@ -183,12 +184,13 @@ def rank_program(g, core, T, topo):
             vop(lambda: V.tensor_scalar(T.off2[:, :], T.yp0[:, 0:16], 256.0, None, A.add))
 
     g.wait_ge(T.sem.yc1, tot["yc1"])
-    send(X, T.res[:, 512:592], T.outb[:, 160:240], "rX")
+    send(Y, T.res[:, 80:160], T.outb[:, 80:160], "rY")
     g.wait_ge(T.sem.yc2, tot["yc2"])
+    send(X, T.res[:, 0:80], T.outb[:, 0:80], "rP")
     g.wait_ge(T.sem.yc3, tot["yc3"])
-    send(Y, T.res[:, 0:160], T.outb[:, 0:160], "rY")
-    g.wait_ge(T.sem.rY, tot["rY"])
-    send(X, T.res[:, 592:672], T.res[:, 0:80], "rD")
+    send(X, T.res[:, 512:592], T.outb[:, 160:240], "rX")
+    g.wait_ge(T.sem.rP, tot["rP"])
+    send(Y, T.res[:, 592:672], T.res[:, 0:80], "rD")
 
     for E in (V, S):
         E.wait_ge(T.sem.v, tot["v"])

@@ -85,21 +85,21 @@ def rank_program(g, core, T, topo):
 
     gop(lambda: g.iota(T.ri[:, :], [[1, 128]], 64, -1))
     g_iota = tot["gq"]
-    vop(lambda: V.memset(T.sg[:, :], 1.0))
-    vop(lambda: V.memset(T.sg[:, 16:32], -1.0))
-    v_sg = vop(lambda: V.memset(T.sg[:, 48:64], -1.0))
+    vop(lambda: V.memset(T.sg[:, :], 0.0))
+    for k, s in ((3, -1.0), (2, 1.0), (1, -1.0), (0, 1.0)):
+        vop(lambda k=k, s=s: V.memset(T.sg[0:16 * k + 16, 16 * k:16 * k + 16], s))
+        if k:
+            vop(lambda k=k: V.memset(T.sg[0:16 * k, 16 * k:16 * k + 16], 0.0))
+    v_sg = tot["v"]
     g.wait_ge(T.sem.v, v_sg)
     gop(lambda: g.affine_select(T.la[:, :], T.sg[:, :], [[1, 64]], A.is_gt, 0.0, 0, -1))
-    gop(lambda: g.affine_select(T.la[:, :], T.la[:, :], [[-16, 4], [0, 16]], A.is_ge, 0.0, 0, 1))
-    gop(lambda: g.affine_select(T.lb[:, :], T.sg[:, :], [[-1, 64]], A.is_ge, 0.0, 0, 1))
-    g_l = gop(lambda: g.affine_select(T.lb[:, :], T.lb[:, :], [[16, 4], [0, 16]], A.is_ge, 0.0, 15, -1))
+    g_l = gop(lambda: g.affine_select(T.lb[:, :], T.sg[:, :], [[-1, 64]], A.is_ge, 0.0, 0, 1))
     for n, val in ((64, kap[3]), (48, kap[2]), (32, kap[1]), (16, kap[0])):
         vop(lambda n=n, val=val: V.memset(T.kcol[0:n, :], float(val)))
     vop(lambda: V.memset(T.m4z[:, 0:1], 0.0))
     vop(lambda: V.memset(T.z16[:, :], 0.0))
     for n, val in ((64, 255.0), (48, 0.0), (32, -1.0), (16, -256.0)):
         vop(lambda n=n, val=val: V.memset(T.b0col[0:n, :], val))
-    vop(lambda: V.memset(T.sw[:, :], 0.0))
     V.wait_ge(T.sem.gq, g_iota)
     vop(lambda: V.tensor_scalar(T.ri2[:, :], T.ri[:, :], 15, None, A.bitwise_and))
     vop(lambda: V.tensor_scalar(T.r1[:, :], T.ri2[:, :], 0, None, A.is_equal))
@@ -110,6 +110,7 @@ def rank_program(g, core, T, topo):
     P.wait_ge(T.sem.gq, g_l)
     inc(P.matmul(T.yp2[0:64, 0:16], T.la[:, :], T.m4z[:, 1:17], True, False), "pi1")
     inc(P.matmul(T.yp2[0:64, 0:16], T.lb[:, :], T.m4z[:, 0:16], False, True), "pi1")
+    vop(lambda: V.memset(T.sw[:, :], 0.0))
     V.wait_ge(T.sem.pi1, tot["pi1"])
     vop(lambda: V.tensor_tensor_scan(T.offk[:, :], T.yp2[0:64, 0:16], T.z16[:, :], T.b0col[:, 0:1], A.add, A.add))
     v_prod = vop(lambda: V.tensor_tensor(T.prod[:, :], T.offk[:, :], T.m4z[:, 1:17], A.mult))
@@ -136,9 +137,9 @@ def rank_program(g, core, T, topo):
     g.wait_ge(T.sem.v, v_sc)
     send(X, T.xin[:, 80:160], T.sw[:, 256:336], "aP")
     send(Y, T.xin[:, 160:240], T.sw[:, 0:80], "aY")
-    send(X, T.xin[:, 0:80], T.sw[:, 176:256], "aX")
     g.wait_ge(T.sem.aP, tot["aP"])
     send(Y, T.xin[:, 240:320], T.xin[:, 80:160], "aD")
+    send(X, T.xin[:, 0:80], T.sw[:, 176:256], "aX")
 
     hp = [T.hp0, T.hp1, T.hp2, T.hp3]
     yp = [T.yp0, T.yp1, T.yp2, T.yp3]

@@ -37,7 +37,7 @@ SCRATCH = {
     "yp2": ("psum", [128, 512], "float32"),
     "yp3": ("psum", [128, 512], "float32"),
 }
-SEMAPHORES = ["sex", "sx", "sw1", "sw2", "sy", "v", "gq", "pi1", "pi2", "pi3",
+SEMAPHORES = ["sex", "sx", "sw1", "sw2", "sy", "v", "v2", "vs", "gi", "gq", "pi1", "pi2", "pi3",
               "mh0", "mh1", "mh2", "mh3", "rh0", "rh1", "rh2", "rh3",
               "my0", "my1", "my2", "my3", "yc0", "yc1", "yc2", "yc3",
               "aP", "aX", "aY", "aD", "rP", "rX", "rY", "rD", "ls", "gv", "ga"]
@@ -65,16 +65,10 @@ def rank_program(g, core, T, topo):
         tot[name] = tot.get(name, 0) + n
         return tot[name]
 
-    def chain(queue, name, make):
-        if tot.get(name, 0):
-            queue.wait_ge(T.sem[name], tot[name])
-        return inc(make(), name)
-
     def vop(make):
-        return chain(V, "v", make)
-
-    def gop(make):
-        return chain(g, "gq", make)
+        if tot.get("v", 0):
+            V.wait_ge(T.sem.v, tot["v"])
+        return inc(make(), "v")
 
     for k in range(4):
         inc((Q if k < 2 else S).dma_start(T.ex4[16 * k:16 * k + 16, :], T.ex[:, :]), "sex", 16)
@@ -83,26 +77,29 @@ def rank_program(g, core, T, topo):
     inc(Q.dma_start(T.w1s[:, :], T.w1[:, :]), "sw1", 16)
     inc(S.dma_start(T.w2s[:, :], T.w2[:, :]), "sw2", 16)
 
-    gop(lambda: g.iota(T.ri[:, :], [[1, 128]], 64, -1))
-    g_iota = tot["gq"]
-    vop(lambda: V.memset(T.sg[:, :], 0.0))
-    for k, s in ((3, -1.0), (2, 1.0), (1, -1.0), (0, 1.0)):
-        vop(lambda k=k, s=s: V.memset(T.sg[0:16 * k + 16, 16 * k:16 * k + 16], s))
-        if k:
-            vop(lambda k=k: V.memset(T.sg[0:16 * k, 16 * k:16 * k + 16], 0.0))
-    v_sg = tot["v"]
-    g.wait_ge(T.sem.v, v_sg)
-    gop(lambda: g.affine_select(T.la[:, :], T.sg[:, :], [[1, 64]], A.is_gt, 0.0, 0, -1))
-    g_l = gop(lambda: g.affine_select(T.lb[:, :], T.sg[:, :], [[-1, 64]], A.is_ge, 0.0, 0, 1))
-    for n, val in ((64, kap[3]), (48, kap[2]), (32, kap[1]), (16, kap[0])):
-        vop(lambda n=n, val=val: V.memset(T.kcol[0:n, :], float(val)))
-    vop(lambda: V.memset(T.m4z[:, 0:1], 0.0))
-    vop(lambda: V.memset(T.z16[:, :], 0.0))
-    for n, val in ((64, 255.0), (48, 0.0), (32, -1.0), (16, -256.0)):
-        vop(lambda n=n, val=val: V.memset(T.b0col[0:n, :], val))
-    V.wait_ge(T.sem.gq, g_iota)
-    vop(lambda: V.tensor_scalar(T.ri2[:, :], T.ri[:, :], 15, None, A.bitwise_and))
-    vop(lambda: V.tensor_scalar(T.r1[:, :], T.ri2[:, :], 0, None, A.is_equal))
+    inc(g.iota(T.ri[:, :], [[1, 128]], 64, -1), "gi")
+    for k, s in enumerate((1.0, -1.0, 1.0, -1.0)):
+        inc(V.memset(T.sg[:, 16 * k:16 * k + 16], s), "vs")
+    cols = ((T.kcol, [float(k) for k in kap]),
+            (T.b0col, [-256.0, -1.0, 0.0, 255.0]),
+            (T.shcol, [0.0, 256.0, 256.0, 512.0]))
+    for buf, val in cols:
+        inc(V.memset(buf[0:32, :], val[1]), "v")
+        inc(V.memset(buf[32:64, :], val[3]), "v")
+    inc(V.memset(T.m4z[:, 0:1], 0.0), "v")
+    inc(V.memset(T.z16[:, :], 0.0), "v")
+    g.wait_ge(T.sem.vs, tot["vs"])
+    inc(g.affine_select(T.la[:, :], T.sg[:, :], [[1, 64]], A.is_gt, 0.0, 0, -1), "gq")
+    inc(g.affine_select(T.lb[:, :], T.sg[:, :], [[-1, 64]], A.is_ge, 0.0, 0, 1), "gq")
+    g.wait_ge(T.sem.gq, tot["gq"])
+    inc(g.affine_select(T.la[:, :], T.la[:, :], [[-16, 4], [0, 16]], A.is_ge, 0.0, 0, 1), "gq")
+    g_l = inc(g.affine_select(T.lb[:, :], T.lb[:, :], [[16, 4], [0, 16]], A.is_ge, 0.0, 15, -1), "gq")
+    V.wait_ge(T.sem.v, tot["v"])
+    for buf, val in cols:
+        inc(V.memset(buf[0:16, :], val[0]), "v")
+        inc(V.memset(buf[32:48, :], val[2]), "v")
+    V.wait_ge(T.sem.gi, tot["gi"])
+    inc(V.tensor_scalar(T.ri2[:, :], T.ri[:, :], 15, None, A.bitwise_and), "v")
 
     V.wait_ge(T.sem.sex, tot["sex"])
     v_m4 = vop(lambda: V.tensor_scalar(T.m4z[:, 1:17], T.ex4[:, :], T.kcol[:, 0:1], None, A.is_equal))
@@ -110,21 +107,22 @@ def rank_program(g, core, T, topo):
     P.wait_ge(T.sem.gq, g_l)
     inc(P.matmul(T.yp2[0:64, 0:16], T.la[:, :], T.m4z[:, 1:17], True, False), "pi1")
     inc(P.matmul(T.yp2[0:64, 0:16], T.lb[:, :], T.m4z[:, 0:16], False, True), "pi1")
-    vop(lambda: V.memset(T.sw[:, :], 0.0))
+    inc(V.memset(T.sw[:, :], 0.0), "v2")
+    v2_r1 = inc(V.tensor_scalar(T.r1[:, :], T.ri2[:, :], 0, None, A.is_equal), "v2")
     V.wait_ge(T.sem.pi1, tot["pi1"])
     vop(lambda: V.tensor_tensor_scan(T.offk[:, :], T.yp2[0:64, 0:16], T.z16[:, :], T.b0col[:, 0:1], A.add, A.add))
     v_prod = vop(lambda: V.tensor_tensor(T.prod[:, :], T.offk[:, :], T.m4z[:, 1:17], A.mult))
     P.wait_ge(T.sem.v, v_prod)
+    P.wait_ge(T.sem.v2, v2_r1)
     inc(P.matmul(T.yp3[:, 0:16], T.r1[:, :], T.prod[:, :], True, True), "pi2")
     V.wait_ge(T.sem.pi2, tot["pi2"])
     vop(lambda: V.tensor_scalar(T.off[:, :], T.yp3[:, 0:16], 256.0, None, A.add))
     V.wait_ge(T.sem.sx, tot["sx"])
+    V.wait_ge(T.sem.v2, v2_r1)
     v_sc = vop(lambda: V.tensor_copy(T.sw[:, 0:512].indirect(T.off[:, 0:16]), T.xs[:, :]))
-    for n, val in ((64, 512.0), (48, 256.0), (16, 0.0)):
-        vop(lambda n=n, val=val: V.memset(T.shcol[0:n, :], val))
-    v_rb = vop(lambda: V.tensor_scalar(T.rb[:, :], T.ri2[:, :], 0, T.shcol[:, 0:1], A.is_equal, A.mult))
-    vop(lambda: V.memset(T.res[:, 160:512], 0.0))
-    vop(lambda: V.memset(T.res[:, 672:1024], 0.0))
+    inc(V.tensor_scalar(T.rb[:, :], T.ri2[:, :], 0, T.shcol[:, 0:1], A.is_equal, A.mult), "v2")
+    inc(V.memset(T.res[:, 160:512], 0.0), "v2")
+    v2_rb = inc(V.memset(T.res[:, 672:1024], 0.0), "v2")
 
     def send(dst, out_ap, in_ap, sem):
         rid, pid = topo.addr(dst, core)
@@ -137,9 +135,9 @@ def rank_program(g, core, T, topo):
     g.wait_ge(T.sem.v, v_sc)
     send(X, T.xin[:, 80:160], T.sw[:, 256:336], "aP")
     send(Y, T.xin[:, 160:240], T.sw[:, 0:80], "aY")
+    send(X, T.xin[:, 0:80], T.sw[:, 176:256], "aX")
     g.wait_ge(T.sem.aP, tot["aP"])
     send(Y, T.xin[:, 240:320], T.xin[:, 80:160], "aD")
-    send(X, T.xin[:, 0:80], T.sw[:, 176:256], "aX")
 
     hp = [T.hp0, T.hp1, T.hp2, T.hp3]
     yp = [T.yp0, T.yp1, T.yp2, T.yp3]
@@ -178,7 +176,7 @@ def rank_program(g, core, T, topo):
         inc(V.tensor_copy(dest, yp[b][:, 0:CAP]), "yc%d" % b)
         if b == 0:
             P.wait_ge(T.sem.yc0, tot["yc0"])
-            P.wait_ge(T.sem.v, v_rb)
+            P.wait_ge(T.sem.v2, v2_rb)
             inc(P.matmul(T.yp0[:, 0:16], T.r1[:, :], T.prod[:, :], True, False), "pi3")
             inc(P.matmul(T.yp0[:, 0:16], T.rb[:, :], T.m4z[:, 1:17], False, True), "pi3")
             V.wait_ge(T.sem.pi3, tot["pi3"])
@@ -195,7 +193,7 @@ def rank_program(g, core, T, topo):
 
     for E in (V, S):
         E.wait_ge(T.sem.v, tot["v"])
-        for name in ("yc0", "rX", "rY", "rD"):
+        for name in ("v2", "yc0", "rX", "rY", "rD"):
             E.wait_ge(T.sem[name], tot[name])
     inc(V.tensor_copy(T.ys[:, 0:128], T.res[:, 80:1104].indirect(T.off2[:, 0:8])), "gv")
     inc(S.activation(T.ys[:, 128:256], T.res[:, 80:1104].indirect(T.off2[:, 8:16]), ActivationFunctionType.Copy), "ga")

@@ -1,32 +1,36 @@
 from concourse.mybir import AluOpType, ActivationFunctionType
 
 CAP = 80
+PITCH = 88
+MID = 172
 SCRATCH = {
-    "ex4": ("sbuf", [64, 16], "int32"),
-    "kcol": ("sbuf", [64, 1], "float32"),
-    "b0col": ("sbuf", [64, 1], "float32"),
-    "shcol": ("sbuf", [64, 1], "float32"),
-    "sg": ("sbuf", [64, 64], "bfloat16"),
-    "la": ("sbuf", [64, 64], "bfloat16"),
-    "lb": ("sbuf", [64, 64], "bfloat16"),
-    "ri": ("sbuf", [64, 128], "int32"),
-    "ri2": ("sbuf", [64, 128], "int32"),
-    "r1": ("sbuf", [64, 128], "bfloat16"),
-    "rb": ("sbuf", [64, 128], "bfloat16"),
-    "m4z": ("sbuf", [64, 17], "bfloat16"),
-    "z16": ("sbuf", [64, 16], "float32"),
-    "offk": ("sbuf", [64, 16], "float32"),
-    "prod": ("sbuf", [64, 16], "bfloat16"),
-    "off": ("sbuf", [128, 16], "uint16"),
+    "exn": ("sbuf", [128, 9], "int32"),
+    "i1": ("sbuf", [128, 128], "int32"),
+    "jj": ("sbuf", [128, 80], "int32"),
+    "k2": ("sbuf", [128, 8], "int32"),
+    "k3": ("sbuf", [128, 8], "int32"),
+    "ri2": ("sbuf", [128, 128], "int32"),
+    "ones": ("sbuf", [128, 128], "bfloat16"),
+    "lt": ("sbuf", [128, 128], "bfloat16"),
+    "idn": ("sbuf", [128, 128], "bfloat16"),
+    "r1": ("sbuf", [128, 128], "bfloat16"),
+    "bm": ("sbuf", [128, 8], "bfloat16"),
+    "m8": ("sbuf", [128, 8], "bfloat16"),
+    "mf": ("sbuf", [128, 8], "float32"),
+    "cs": ("sbuf", [128, 8], "float32"),
+    "rk": ("sbuf", [128, 64], "bfloat16"),
     "off2": ("sbuf", [128, 16], "uint16"),
     "xs": ("sbuf", [128, 256], "bfloat16"),
-    "sw": ("sbuf", [128, 512], "bfloat16"),
+    "xt": ("sbuf", [128, 256], "bfloat16"),
+    "sel": ("sbuf", [128, 640], "bfloat16"),
+    "xb": ("sbuf", [128, 320], "bfloat16"),
     "xin": ("sbuf", [128, 320], "bfloat16"),
     "w1s": ("sbuf", [128, 1024], "bfloat16"),
     "w2s": ("sbuf", [128, 1024], "bfloat16"),
     "hs": ("sbuf", [128, 2560], "bfloat16"),
     "outb": ("sbuf", [128, 240], "bfloat16"),
-    "res": ("sbuf", [128, 1104], "bfloat16"),
+    "stg": ("sbuf", [128, 80], "bfloat16"),
+    "res": ("sbuf", [128, 352], "bfloat16"),
     "ys": ("sbuf", [128, 256], "bfloat16"),
     "hp0": ("psum", [128, 512], "float32"),
     "hp1": ("psum", [128, 512], "float32"),
@@ -37,7 +41,7 @@ SCRATCH = {
     "yp2": ("psum", [128, 512], "float32"),
     "yp3": ("psum", [128, 512], "float32"),
 }
-SEMAPHORES = ["sex", "sx", "sw1", "sw2", "sy", "v", "v2", "vs", "gi", "gq", "pi1", "pi2", "pi3",
+SEMAPHORES = ["sex", "sx", "sw1", "sw2", "sy", "v", "gi", "gq", "pc1", "pc2", "pt", "pd", "sc", "pi3",
               "mh0", "mh1", "mh2", "mh3", "rh0", "rh1", "rh2", "rh3",
               "my0", "my1", "my2", "my3", "yc0", "yc1", "yc2", "yc3",
               "aP", "aX", "aY", "aD", "rP", "rX", "rY", "rD", "ls", "gv", "ga"]
@@ -48,12 +52,13 @@ def rank_program(g, core, T, topo):
     if rank is None:
         return
     A = AluOpType
+    F = ActivationFunctionType
     V, S, P, Q = g.vector, g.scalar, g.tensor, g.sync
     others = [c for c in T.cores if c != core]
     X = [c for c in others if topo.same_plane(core, c)][0]
     D = [c for c in others if not topo.may_write(core, c)][0]
     Y = [c for c in others if c != X and c != D][0]
-    kap = [T.rank_of(Y), T.rank_of(X), T.rank_of(D), rank]
+    kap = [T.rank_of(D), T.rank_of(Y), T.rank_of(X), rank]
 
     def engines(src, dst):
         return bin(topo.mask(src, dst)).count("1")
@@ -65,64 +70,88 @@ def rank_program(g, core, T, topo):
         tot[name] = tot.get(name, 0) + n
         return tot[name]
 
-    def vop(make):
-        if tot.get("v", 0):
-            V.wait_ge(T.sem.v, tot["v"])
-        return inc(make(), "v")
-
-    for k in range(4):
-        inc((Q if k < 2 else S).dma_start(T.ex4[16 * k:16 * k + 16, :], T.ex[:, :]), "sex", 16)
+    for a in range(8):
+        inc((Q if a < 4 else S).dma_start(T.exn[16 * a:16 * a + 16, :], T.ex[:, a:a + 9]), "sex", 16)
     inc(Q.dma_start(T.xs[0:64, :], T.x[0:64, :]), "sx", 16)
     inc(S.dma_start(T.xs[64:128, :], T.x[64:128, :]), "sx", 16)
     inc(Q.dma_start(T.w1s[:, :], T.w1[:, :]), "sw1", 16)
     inc(S.dma_start(T.w2s[:, :], T.w2[:, :]), "sw2", 16)
 
-    inc(g.iota(T.ri[:, :], [[1, 128]], 64, -1), "gi")
-    for k, s in enumerate((1.0, -1.0, 1.0, -1.0)):
-        inc(V.memset(T.sg[:, 16 * k:16 * k + 16], s), "vs")
-    cols = ((T.kcol, [float(k) for k in kap]),
-            (T.b0col, [-256.0, -1.0, 0.0, 255.0]),
-            (T.shcol, [0.0, 256.0, 256.0, 512.0]))
-    for buf, val in cols:
-        inc(V.memset(buf[0:32, :], val[1]), "v")
-        inc(V.memset(buf[32:64, :], val[3]), "v")
-    inc(V.memset(T.m4z[:, 0:1], 0.0), "v")
-    inc(V.memset(T.z16[:, :], 0.0), "v")
-    g.wait_ge(T.sem.vs, tot["vs"])
-    inc(g.affine_select(T.la[:, :], T.sg[:, :], [[1, 64]], A.is_gt, 0.0, 0, -1), "gq")
-    inc(g.affine_select(T.lb[:, :], T.sg[:, :], [[-1, 64]], A.is_ge, 0.0, 0, 1), "gq")
-    g.wait_ge(T.sem.gq, tot["gq"])
-    inc(g.affine_select(T.la[:, :], T.la[:, :], [[-16, 4], [0, 16]], A.is_ge, 0.0, 0, 1), "gq")
-    g_l = inc(g.affine_select(T.lb[:, :], T.lb[:, :], [[16, 4], [0, 16]], A.is_ge, 0.0, 15, -1), "gq")
-    V.wait_ge(T.sem.v, tot["v"])
-    for buf, val in cols:
-        inc(V.memset(buf[0:16, :], val[0]), "v")
-        inc(V.memset(buf[32:48, :], val[2]), "v")
+    inc(g.iota(T.i1[:, :], [[1, 128]], 0, -1), "gi")
+    g_j = inc(g.iota(T.jj[:, :], [[1, 80]], 0, 0), "gq")
+    g_k = inc(g.iota(T.k2[:, :], [[-16, 8]], 0, 1), "gq")
+    inc(V.memset(T.ones[:, :], 1.0), "v")
     V.wait_ge(T.sem.gi, tot["gi"])
-    inc(V.tensor_scalar(T.ri2[:, :], T.ri[:, :], 15, None, A.bitwise_and), "v")
+    inc(V.tensor_scalar(T.lt[:, :], T.i1[:, :], 0, None, A.is_gt), "v")
+    inc(V.tensor_scalar(T.idn[:, :], T.i1[:, :], 0, None, A.is_equal), "v")
+
+    def onehot(buf, k):
+        return inc(V.tensor_scalar(buf[:, k:8:4], T.exn[:, 0:9:8], float(kap[k]), None, A.is_equal), "v")
 
     V.wait_ge(T.sem.sex, tot["sex"])
-    v_m4 = vop(lambda: V.tensor_scalar(T.m4z[:, 1:17], T.ex4[:, :], T.kcol[:, 0:1], None, A.is_equal))
-    P.wait_ge(T.sem.v, v_m4)
-    P.wait_ge(T.sem.gq, g_l)
-    inc(P.matmul(T.yp2[0:64, 0:16], T.la[:, :], T.m4z[:, 1:17], True, False), "pi1")
-    inc(P.matmul(T.yp2[0:64, 0:16], T.lb[:, :], T.m4z[:, 0:16], False, True), "pi1")
-    inc(V.memset(T.sw[:, :], 0.0), "v2")
-    v2_r1 = inc(V.tensor_scalar(T.r1[:, :], T.ri2[:, :], 0, None, A.is_equal), "v2")
-    V.wait_ge(T.sem.pi1, tot["pi1"])
-    vop(lambda: V.tensor_tensor_scan(T.offk[:, :], T.yp2[0:64, 0:16], T.z16[:, :], T.b0col[:, 0:1], A.add, A.add))
-    v_prod = vop(lambda: V.tensor_tensor(T.prod[:, :], T.offk[:, :], T.m4z[:, 1:17], A.mult))
-    P.wait_ge(T.sem.v, v_prod)
-    P.wait_ge(T.sem.v2, v2_r1)
-    inc(P.matmul(T.yp3[:, 0:16], T.r1[:, :], T.prod[:, :], True, True), "pi2")
-    V.wait_ge(T.sem.pi2, tot["pi2"])
-    vop(lambda: V.tensor_scalar(T.off[:, :], T.yp3[:, 0:16], 256.0, None, A.add))
-    V.wait_ge(T.sem.sx, tot["sx"])
-    V.wait_ge(T.sem.v2, v2_r1)
-    v_sc = vop(lambda: V.tensor_copy(T.sw[:, 0:512].indirect(T.off[:, 0:16]), T.xs[:, :]))
-    inc(V.tensor_scalar(T.rb[:, :], T.ri2[:, :], 0, T.shcol[:, 0:1], A.is_equal, A.mult), "v2")
-    inc(V.memset(T.res[:, 160:512], 0.0), "v2")
-    v2_rb = inc(V.memset(T.res[:, 672:1024], 0.0), "v2")
+    v_md = onehot(T.m8, 0)
+    v_fd = onehot(T.mf, 0)
+    for k in range(1, 4):
+        v_mr = onehot(T.m8, k)
+    for k in range(1, 4):
+        v_fr = onehot(T.mf, k)
+    P.wait_ge(T.sem.v, v_md)
+    inc(P.matmul(T.yp2[:, 0:1], T.lt[:, :], T.m8[:, 0:1], True, True), "pc1")
+    inc(P.matmul(T.yp2[:, 1:2], T.lt[:, :], T.m8[:, 4:5], True, False), "pc1")
+    inc(P.matmul(T.yp2[:, 1:2], T.ones[:, :], T.m8[:, 0:1], False, True), "pc1")
+    P.wait_ge(T.sem.sx, tot["sx"])
+    inc(P.matmul(T.hp0[:, 0:128], T.xs[:, 0:128], T.idn[:, :], True, True), "pt")
+    inc(P.matmul(T.hp1[:, 0:128], T.xs[:, 128:256], T.idn[:, :], True, True), "pt")
+    P.wait_ge(T.sem.v, v_mr)
+    inc(P.matmul(T.yp3[:, 0:3], T.lt[:, :], T.m8[:, 1:4], True, True), "pc2")
+    inc(P.matmul(T.yp3[:, 3:6], T.lt[:, :], T.m8[:, 5:8], True, False), "pc2")
+    inc(P.matmul(T.yp3[:, 3:6], T.ones[:, :], T.m8[:, 1:4], False, True), "pc2")
+    for h, bank in enumerate((T.hp0, T.hp1)):
+        S.wait_ge(T.sem.pt, h + 1)
+        s_xt = inc(S.activation(T.xt[:, 128 * h:128 * h + 128], bank[:, 0:128], F.Copy), "sc")
+
+    def place(k, h):
+        return T.yp2[:, h:h + 1] if k == 0 else T.yp3[:, 3 * h + k - 1:3 * h + k]
+
+    v_sel = []
+    V.wait_ge(T.sem.gq, g_j)
+    for k in range(4):
+        if k < 2:
+            V.wait_ge(T.sem.v, v_fd if k == 0 else v_fr)
+            V.wait_ge(T.sem["pc1" if k == 0 else "pc2"], 3)
+        for h in range(2):
+            c = 160 * k + 80 * h
+            n = inc(V.tensor_scalar(T.sel[:, c:c + 80], T.jj[:, :], place(k, h), T.mf[:, 4 * h + k:4 * h + k + 1],
+                                    A.is_equal, A.mult), "v")
+        v_sel.append(n)
+    dps = [T.hp2, T.hp3, T.yp1, T.yp0]
+    s_cp = []
+    P.wait_ge(T.sem.sc, s_xt)
+    for k in range(4):
+        P.wait_ge(T.sem.v, v_sel[k])
+        for h in range(2):
+            c = 160 * k + 80 * h
+            n = inc(P.matmul(dps[k][:, 0:CAP], T.xt[:, 128 * h:128 * h + 128], T.sel[:, c:c + 80], h == 0, h == 1), "pd")
+        S.wait_ge(T.sem.pd, n)
+        s_cp.append(inc(S.activation(T.xb[:, CAP * k:CAP * k + CAP], dps[k][:, 0:CAP], F.Copy), "sc"))
+
+    inc(V.tensor_scalar(T.cs[:, 0:8:4], T.yp2[:, 0:2], float(CAP), float(-MID), A.min, A.add), "v")
+    for k in range(1, 4):
+        inc(V.tensor_scalar(T.cs[:, k:8:4], T.yp3[:, k - 1:6:3], float(CAP), float(PITCH * k - MID), A.min, A.add), "v")
+    V.wait_ge(T.sem.gq, g_k)
+    inc(V.tensor_scalar(T.k3[:, :], T.k2[:, :], 4, None, A.arith_shift_right), "v")
+    inc(V.tensor_scalar(T.ri2[:, :], T.i1[:, :], 15, None, A.bitwise_and), "v")
+    for k in range(4):
+        inc(V.memset(T.res[:, PITCH * k + CAP:PITCH * k + PITCH], 0.0), "v")
+    V.wait_ge(T.sem.v, tot["v"])
+    inc(V.tensor_scalar(T.bm[:, :], T.k3[:, :], 0, None, A.is_equal), "v")
+    inc(V.tensor_scalar(T.r1[:, :], T.ri2[:, :], 0, None, A.is_equal), "v")
+    V.wait_ge(T.sem.v, tot["v"])
+    for k in range(4):
+        for h in range(2):
+            i = 4 * h + k
+            v_rk = inc(V.tensor_scalar(T.rk[:, 16 * k + 8 * h:16 * k + 8 * h + 8], T.bm[:, :], T.cs[:, i:i + 1],
+                                       T.mf[:, i:i + 1], A.mult, A.mult), "v")
 
     def send(dst, out_ap, in_ap, sem):
         rid, pid = topo.addr(dst, core)
@@ -132,20 +161,23 @@ def rank_program(g, core, T, topo):
     for name, src in (("aP", X), ("aX", X), ("aY", Y), ("aD", Y), ("rP", X), ("rX", X), ("rY", Y), ("rD", Y)):
         tot[name] = engines(src, core)
 
-    g.wait_ge(T.sem.v, v_sc)
-    send(X, T.xin[:, 80:160], T.sw[:, 256:336], "aP")
-    send(Y, T.xin[:, 160:240], T.sw[:, 0:80], "aY")
-    send(X, T.xin[:, 0:80], T.sw[:, 176:256], "aX")
+    g.wait_ge(T.sem.sc, s_cp[0])
+    send(X, T.xin[:, 80:160], T.xb[:, 0:80], "aP")
+    g.wait_ge(T.sem.sc, s_cp[1])
+    send(Y, T.xin[:, 160:240], T.xb[:, 80:160], "aY")
+    g.wait_ge(T.sem.sc, s_cp[2])
+    send(X, T.xin[:, 0:80], T.xb[:, 160:240], "aX")
     g.wait_ge(T.sem.aP, tot["aP"])
     send(Y, T.xin[:, 240:320], T.xin[:, 80:160], "aD")
 
     hp = [T.hp0, T.hp1, T.hp2, T.hp3]
     yp = [T.yp0, T.yp1, T.yp2, T.yp3]
-    blocks = [(T.sw[:, 432:512], None, T.res[:, 1024:1104]),
+    blocks = [(T.xb[:, 240:320], None, T.res[:, 3 * PITCH:3 * PITCH + CAP]),
               (T.xin[:, 160:240], "aY", T.outb[:, 80:160]),
               (T.xin[:, 240:320], "aD", T.outb[:, 0:80]),
               (T.xin[:, 0:80], "aX", T.outb[:, 160:240])]
-    P.wait_ge(T.sem.v, v_sc)
+    v_off2 = 0
+    P.wait_ge(T.sem.sc, s_cp[3])
     P.wait_ge(T.sem.sw1, tot["sw1"])
     for b, (rhs, arr, dest) in enumerate(blocks):
         if arr:
@@ -163,9 +195,11 @@ def rank_program(g, core, T, topo):
             if i % 2 == 0:
                 inc(V.tensor_scalar(h, hp[i][:, 0:160], 0.0, None, A.max), "rh%d" % i)
             else:
-                inc(S.activation(h, hp[i][:, 0:160], ActivationFunctionType.Relu), "rh%d" % i)
+                inc(S.activation(h, hp[i][:, 0:160], F.Relu), "rh%d" % i)
         if b == 0:
             P.wait_ge(T.sem.sw2, tot["sw2"])
+        if b == 3:
+            P.wait_ge(T.sem.v, v_off2)
         for i in range(4):
             P.wait_ge(T.sem["rh%d" % i], b + 1)
             for f in (2 * i, 2 * i + 1):
@@ -175,28 +209,26 @@ def rank_program(g, core, T, topo):
         V.wait_ge(T.sem["my%d" % b], tot["my%d" % b])
         inc(V.tensor_copy(dest, yp[b][:, 0:CAP]), "yc%d" % b)
         if b == 0:
-            P.wait_ge(T.sem.yc0, tot["yc0"])
-            P.wait_ge(T.sem.v2, v2_rb)
-            inc(P.matmul(T.yp0[:, 0:16], T.r1[:, :], T.prod[:, :], True, False), "pi3")
-            inc(P.matmul(T.yp0[:, 0:16], T.rb[:, :], T.m4z[:, 1:17], False, True), "pi3")
+            P.wait_ge(T.sem.v, v_rk)
+            for k in range(4):
+                inc(P.matmul(T.yp3[:, 16:32], T.r1[:, :], T.rk[:, 16 * k:16 * k + 16], k == 0, k == 3), "pi3")
             V.wait_ge(T.sem.pi3, tot["pi3"])
-            vop(lambda: V.tensor_scalar(T.off2[:, :], T.yp0[:, 0:16], 256.0, None, A.add))
+            v_off2 = inc(V.tensor_scalar(T.off2[:, :], T.yp3[:, 16:32], float(MID), None, A.add), "v")
 
     g.wait_ge(T.sem.yc1, tot["yc1"])
-    send(Y, T.res[:, 80:160], T.outb[:, 80:160], "rY")
+    send(Y, T.res[:, PITCH:PITCH + CAP], T.outb[:, 80:160], "rY")
     g.wait_ge(T.sem.yc2, tot["yc2"])
-    send(X, T.res[:, 0:80], T.outb[:, 0:80], "rP")
+    send(X, T.stg[:, :], T.outb[:, 0:80], "rP")
     g.wait_ge(T.sem.yc3, tot["yc3"])
-    send(X, T.res[:, 512:592], T.outb[:, 160:240], "rX")
+    send(X, T.res[:, 2 * PITCH:2 * PITCH + CAP], T.outb[:, 160:240], "rX")
     g.wait_ge(T.sem.rP, tot["rP"])
-    send(Y, T.res[:, 592:672], T.res[:, 0:80], "rD")
+    send(Y, T.res[:, 0:CAP], T.stg[:, :], "rD")
 
     for E in (V, S):
-        E.wait_ge(T.sem.v, tot["v"])
-        for name in ("v2", "yc0", "rX", "rY", "rD"):
+        for name in ("v", "yc0", "rX", "rY", "rD"):
             E.wait_ge(T.sem[name], tot[name])
-    inc(V.tensor_copy(T.ys[:, 0:128], T.res[:, 80:1104].indirect(T.off2[:, 0:8])), "gv")
-    inc(S.activation(T.ys[:, 128:256], T.res[:, 80:1104].indirect(T.off2[:, 8:16]), ActivationFunctionType.Copy), "ga")
+    inc(V.tensor_copy(T.ys[:, 0:128], T.res[:, 0:4 * PITCH].indirect(T.off2[:, 0:8])), "gv")
+    inc(S.activation(T.ys[:, 128:256], T.res[:, 0:4 * PITCH].indirect(T.off2[:, 8:16]), F.Copy), "ga")
     Q.wait_ge(T.sem.gv, tot["gv"])
     Q.wait_ge(T.sem.ga, tot["ga"])
     inc(Q.dma_start(T.y[:, :], T.ys[:, :]), "sy", 16)

@@ -44,24 +44,40 @@ SCRATCH = {
 SEMAPHORES = ["sex", "sx", "sw1", "sw2", "sy", "v", "gi", "gq", "pc1", "pc2", "pt", "pd", "sc", "pi3",
               "mh0", "mh1", "mh2", "mh3", "rh0", "rh1", "rh2", "rh3",
               "my0", "my1", "my2", "my3", "yc0", "yc1", "yc2", "yc3",
-              "aP", "aX", "aY", "aD", "rP", "rX", "rY", "rD", "ls", "gv", "ga"]
+              "aP", "aX", "aY", "aD", "rP", "rX", "rY", "rD", "ls", "gv", "ga", "aE", "aO"]
 
 
 def rank_program(g, core, T, topo):
-    rank = T.rank_of(core)
-    if rank is None:
-        return
     A = AluOpType
     F = ActivationFunctionType
     V, S, P, Q = g.vector, g.scalar, g.tensor, g.sync
-    others = [c for c in T.cores if c != core]
-    X = [c for c in others if topo.same_plane(core, c)][0]
-    D = [c for c in others if not topo.may_write(core, c)][0]
+
+    def aide_of(r):
+        world = range(topo.CORES_PER_HOST * (1 + max(topo.host(c) for c in T.cores)))
+        return [c for c in world if c not in T.cores and topo.host(c) == topo.host(r) and topo.chip(c) == topo.chip(r)
+                and topo.die(c) == topo.die(r)][0]
+
+    if T.rank_of(core) is not None:
+        boss = core
+    else:
+        mine = [r for r in T.cores if topo.host(r) == topo.host(core) and topo.chip(r) == topo.chip(core)
+                and aide_of(r) == core]
+        if not mine:
+            return
+        boss = mine[0]
+    aide = aide_of(boss)
+    others = [c for c in T.cores if c != boss]
+    X = [c for c in others if topo.same_plane(boss, c)][0]
+    D = [c for c in others if not topo.may_write(boss, c)][0]
     Y = [c for c in others if c != X and c != D][0]
-    kap = [T.rank_of(D), T.rank_of(Y), T.rank_of(X), rank]
+    kap = [T.rank_of(D), T.rank_of(Y), T.rank_of(X), T.rank_of(boss)]
+    ex_mask = topo.mask(boss, aide) & topo.mask(boss, X)
+
+    def bits(m):
+        return bin(m).count("1")
 
     def engines(src, dst):
-        return bin(topo.mask(src, dst)).count("1")
+        return bits(topo.mask(src, dst))
 
     tot = {}
 
@@ -69,6 +85,60 @@ def rank_program(g, core, T, topo):
         ins.then_inc(T.sem[name], n)
         tot[name] = tot.get(name, 0) + n
         return tot[name]
+
+    def onehot(buf, k):
+        return inc(V.tensor_scalar(buf[:, k:8:4], T.exn[:, 0:9:8], float(kap[k]), None, A.is_equal), "v")
+
+    def send(dst, out_ap, in_ap, sem, mask=None):
+        rid, pid = topo.addr(dst, core)
+        m = topo.mask(core, dst) if mask is None else mask
+        g.remote_dma(out_ap, in_ap, T.sem[sem], T.sem.ls, pid, rid, m)
+        tot["ls"] = tot.get("ls", 0) + bits(m)
+
+    def finish():
+        for name in SEMAPHORES:
+            if tot.get(name, 0):
+                g.wait_ge(T.sem[name], tot[name])
+
+    if core != boss:
+        inc(g.iota(T.i1[:, :], [[1, 128]], 0, -1), "gi")
+        inc(g.iota(T.k2[:, :], [[-16, 8]], 0, 1), "gi")
+        inc(V.memset(T.ones[:, :], 1.0), "v")
+        V.wait_ge(T.sem.gi, tot["gi"])
+        inc(V.tensor_scalar(T.lt[:, :], T.i1[:, :], 0, None, A.is_gt), "v")
+        inc(V.tensor_scalar(T.k3[:, :], T.k2[:, :], 4, None, A.arith_shift_right), "v")
+        inc(V.tensor_scalar(T.ri2[:, :], T.i1[:, :], 15, None, A.bitwise_and), "v")
+        V.wait_ge(T.sem.v, tot["v"])
+        inc(V.tensor_scalar(T.bm[:, :], T.k3[:, :], 0, None, A.is_equal), "v")
+        inc(V.tensor_scalar(T.r1[:, :], T.ri2[:, :], 0, None, A.is_equal), "v")
+        tot["aE"] = bits(ex_mask)
+        V.wait_ge(T.sem.aE, tot["aE"])
+        for k in range(4):
+            onehot(T.m8, k)
+        for k in range(4):
+            onehot(T.mf, k)
+        P.wait_ge(T.sem.v, tot["v"])
+        inc(P.matmul(T.yp2[:, 0:4], T.lt[:, :], T.m8[:, 0:4], True, True), "pc1")
+        inc(P.matmul(T.yp2[:, 4:8], T.lt[:, :], T.m8[:, 4:8], True, False), "pc1")
+        inc(P.matmul(T.yp2[:, 4:8], T.ones[:, :], T.m8[:, 0:4], False, True), "pc1")
+        V.wait_ge(T.sem.pc1, tot["pc1"])
+        for k in range(4):
+            inc(V.tensor_scalar(T.cs[:, k:8:4], T.yp2[:, k:8:4], float(CAP), float(PITCH * k - MID), A.min, A.add), "v")
+        V.wait_ge(T.sem.v, tot["v"])
+        for k in range(4):
+            for h in range(2):
+                i = 4 * h + k
+                inc(V.tensor_scalar(T.rk[:, 16 * k + 8 * h:16 * k + 8 * h + 8], T.bm[:, :], T.cs[:, i:i + 1],
+                                    T.mf[:, i:i + 1], A.mult, A.mult), "v")
+        P.wait_ge(T.sem.v, tot["v"])
+        for k in range(4):
+            inc(P.matmul(T.yp3[:, 0:16], T.r1[:, :], T.rk[:, 16 * k:16 * k + 16], k == 0, k == 3), "pi3")
+        V.wait_ge(T.sem.pi3, tot["pi3"])
+        inc(V.tensor_scalar(T.off2[:, :], T.yp3[:, 0:16], float(MID), None, A.add), "v")
+        g.wait_ge(T.sem.v, tot["v"])
+        send(boss, T.off2[:, :], T.off2[:, :], "aO")
+        finish()
+        return
 
     for a in range(8):
         inc((Q if a < 4 else S).dma_start(T.exn[16 * a:16 * a + 16, :], T.ex[:, a:a + 9]), "sex", 16)
@@ -79,14 +149,13 @@ def rank_program(g, core, T, topo):
 
     inc(g.iota(T.i1[:, :], [[1, 128]], 0, -1), "gi")
     g_j = inc(g.iota(T.jj[:, :], [[1, 80]], 0, 0), "gq")
-    g_k = inc(g.iota(T.k2[:, :], [[-16, 8]], 0, 1), "gq")
     inc(V.memset(T.ones[:, :], 1.0), "v")
     V.wait_ge(T.sem.gi, tot["gi"])
     inc(V.tensor_scalar(T.lt[:, :], T.i1[:, :], 0, None, A.is_gt), "v")
     inc(V.tensor_scalar(T.idn[:, :], T.i1[:, :], 0, None, A.is_equal), "v")
 
-    def onehot(buf, k):
-        return inc(V.tensor_scalar(buf[:, k:8:4], T.exn[:, 0:9:8], float(kap[k]), None, A.is_equal), "v")
+    g.wait_ge(T.sem.sex, tot["sex"])
+    send(aide, T.exn[:, :], T.exn[:, :], "aE", ex_mask)
 
     V.wait_ge(T.sem.sex, tot["sex"])
     v_md = onehot(T.m8, 0)
@@ -135,30 +204,10 @@ def rank_program(g, core, T, topo):
         S.wait_ge(T.sem.pd, n)
         s_cp.append(inc(S.activation(T.xb[:, CAP * k:CAP * k + CAP], dps[k][:, 0:CAP], F.Copy), "sc"))
 
-    inc(V.tensor_scalar(T.cs[:, 0:8:4], T.yp2[:, 0:2], float(CAP), float(-MID), A.min, A.add), "v")
-    for k in range(1, 4):
-        inc(V.tensor_scalar(T.cs[:, k:8:4], T.yp3[:, k - 1:6:3], float(CAP), float(PITCH * k - MID), A.min, A.add), "v")
-    V.wait_ge(T.sem.gq, g_k)
-    inc(V.tensor_scalar(T.k3[:, :], T.k2[:, :], 4, None, A.arith_shift_right), "v")
-    inc(V.tensor_scalar(T.ri2[:, :], T.i1[:, :], 15, None, A.bitwise_and), "v")
     for k in range(4):
         inc(V.memset(T.res[:, PITCH * k + CAP:PITCH * k + PITCH], 0.0), "v")
-    V.wait_ge(T.sem.v, tot["v"])
-    inc(V.tensor_scalar(T.bm[:, :], T.k3[:, :], 0, None, A.is_equal), "v")
-    inc(V.tensor_scalar(T.r1[:, :], T.ri2[:, :], 0, None, A.is_equal), "v")
-    V.wait_ge(T.sem.v, tot["v"])
-    for k in range(4):
-        for h in range(2):
-            i = 4 * h + k
-            v_rk = inc(V.tensor_scalar(T.rk[:, 16 * k + 8 * h:16 * k + 8 * h + 8], T.bm[:, :], T.cs[:, i:i + 1],
-                                       T.mf[:, i:i + 1], A.mult, A.mult), "v")
 
-    def send(dst, out_ap, in_ap, sem):
-        rid, pid = topo.addr(dst, core)
-        g.remote_dma(out_ap, in_ap, T.sem[sem], T.sem.ls, pid, rid, topo.mask(core, dst))
-        tot["ls"] = tot.get("ls", 0) + engines(core, dst)
-
-    for name, src in (("aP", X), ("aX", X), ("aY", Y), ("aD", Y), ("rP", X), ("rX", X), ("rY", Y), ("rD", Y)):
+    for name, src in (("aP", X), ("aX", X), ("aY", Y), ("aD", Y), ("rP", X), ("rX", X), ("rY", Y), ("rD", Y), ("aO", aide)):
         tot[name] = engines(src, core)
 
     g.wait_ge(T.sem.sc, s_cp[0])
@@ -176,7 +225,6 @@ def rank_program(g, core, T, topo):
               (T.xin[:, 160:240], "aY", T.outb[:, 80:160]),
               (T.xin[:, 240:320], "aD", T.outb[:, 0:80]),
               (T.xin[:, 0:80], "aX", T.outb[:, 160:240])]
-    v_off2 = 0
     P.wait_ge(T.sem.sc, s_cp[3])
     P.wait_ge(T.sem.sw1, tot["sw1"])
     for b, (rhs, arr, dest) in enumerate(blocks):
@@ -198,8 +246,6 @@ def rank_program(g, core, T, topo):
                 inc(S.activation(h, hp[i][:, 0:160], F.Relu), "rh%d" % i)
         if b == 0:
             P.wait_ge(T.sem.sw2, tot["sw2"])
-        if b == 3:
-            P.wait_ge(T.sem.v, v_off2)
         for i in range(4):
             P.wait_ge(T.sem["rh%d" % i], b + 1)
             for f in (2 * i, 2 * i + 1):
@@ -208,12 +254,6 @@ def rank_program(g, core, T, topo):
                     "my%d" % b)
         V.wait_ge(T.sem["my%d" % b], tot["my%d" % b])
         inc(V.tensor_copy(dest, yp[b][:, 0:CAP]), "yc%d" % b)
-        if b == 0:
-            P.wait_ge(T.sem.v, v_rk)
-            for k in range(4):
-                inc(P.matmul(T.yp3[:, 16:32], T.r1[:, :], T.rk[:, 16 * k:16 * k + 16], k == 0, k == 3), "pi3")
-            V.wait_ge(T.sem.pi3, tot["pi3"])
-            v_off2 = inc(V.tensor_scalar(T.off2[:, :], T.yp3[:, 16:32], float(MID), None, A.add), "v")
 
     g.wait_ge(T.sem.yc1, tot["yc1"])
     send(Y, T.res[:, PITCH:PITCH + CAP], T.outb[:, 80:160], "rY")
@@ -225,14 +265,11 @@ def rank_program(g, core, T, topo):
     send(Y, T.res[:, 0:CAP], T.stg[:, :], "rD")
 
     for E in (V, S):
-        for name in ("v", "yc0", "rX", "rY", "rD"):
+        for name in ("v", "yc0", "aO", "rX", "rY", "rD"):
             E.wait_ge(T.sem[name], tot[name])
     inc(V.tensor_copy(T.ys[:, 0:128], T.res[:, 0:4 * PITCH].indirect(T.off2[:, 0:8])), "gv")
     inc(S.activation(T.ys[:, 128:256], T.res[:, 0:4 * PITCH].indirect(T.off2[:, 8:16]), F.Copy), "ga")
     Q.wait_ge(T.sem.gv, tot["gv"])
     Q.wait_ge(T.sem.ga, tot["ga"])
     inc(Q.dma_start(T.y[:, :], T.ys[:, :]), "sy", 16)
-
-    for name in SEMAPHORES:
-        if tot.get(name, 0):
-            g.wait_ge(T.sem[name], tot[name])
+    finish()

from concourse.mybir import AluOpType, ActivationFunctionType

CAP = 80
PITCH = 88
MID = 172
SCRATCH = {
    "exn": ("sbuf", [128, 9], "int32"),
    "i1": ("sbuf", [128, 128], "int32"),
    "jj": ("sbuf", [128, 80], "int32"),
    "k2": ("sbuf", [128, 8], "int32"),
    "k3": ("sbuf", [128, 8], "int32"),
    "ri2": ("sbuf", [128, 128], "int32"),
    "ones": ("sbuf", [128, 128], "bfloat16"),
    "lt": ("sbuf", [128, 128], "bfloat16"),
    "idn": ("sbuf", [128, 128], "bfloat16"),
    "r1": ("sbuf", [128, 128], "bfloat16"),
    "bm": ("sbuf", [128, 8], "bfloat16"),
    "m8": ("sbuf", [128, 8], "bfloat16"),
    "mf": ("sbuf", [128, 8], "float32"),
    "cs": ("sbuf", [128, 8], "float32"),
    "rk": ("sbuf", [128, 64], "bfloat16"),
    "off2": ("sbuf", [128, 16], "uint16"),
    "xs": ("sbuf", [128, 256], "bfloat16"),
    "xt": ("sbuf", [128, 256], "bfloat16"),
    "sel": ("sbuf", [128, 640], "bfloat16"),
    "xb": ("sbuf", [128, 320], "bfloat16"),
    "xin": ("sbuf", [128, 320], "bfloat16"),
    "w1s": ("sbuf", [128, 1024], "bfloat16"),
    "w2s": ("sbuf", [128, 1024], "bfloat16"),
    "hs": ("sbuf", [128, 2560], "bfloat16"),
    "outb": ("sbuf", [128, 240], "bfloat16"),
    "stg": ("sbuf", [128, 80], "bfloat16"),
    "res": ("sbuf", [128, 352], "bfloat16"),
    "ys": ("sbuf", [128, 256], "bfloat16"),
    "hp0": ("psum", [128, 512], "float32"),
    "hp1": ("psum", [128, 512], "float32"),
    "hp2": ("psum", [128, 512], "float32"),
    "hp3": ("psum", [128, 512], "float32"),
    "yp0": ("psum", [128, 512], "float32"),
    "yp1": ("psum", [128, 512], "float32"),
    "yp2": ("psum", [128, 512], "float32"),
    "yp3": ("psum", [128, 512], "float32"),
}
SEMAPHORES = ["sex", "sx", "sw1", "sw2", "sy", "v", "gi", "gq", "pc1", "pc2", "pt", "pd", "sc", "pi3",
              "mh0", "mh1", "mh2", "mh3", "rh0", "rh1", "rh2", "rh3",
              "my0", "my1", "my2", "my3", "yc0", "yc1", "yc2", "yc3",
              "aP", "aX", "aY", "aD", "rP", "rX", "rY", "rD", "ls", "gv", "ga", "aE", "aO"]


def rank_program(g, core, T, topo):
    A = AluOpType
    F = ActivationFunctionType
    V, S, P, Q = g.vector, g.scalar, g.tensor, g.sync

    def aide_of(r):
        world = range(topo.CORES_PER_HOST * (1 + max(topo.host(c) for c in T.cores)))
        return [c for c in world if c not in T.cores and topo.host(c) == topo.host(r) and topo.chip(c) == topo.chip(r)
                and topo.die(c) == topo.die(r)][0]

    if T.rank_of(core) is not None:
        boss = core
    else:
        mine = [r for r in T.cores if topo.host(r) == topo.host(core) and topo.chip(r) == topo.chip(core)
                and aide_of(r) == core]
        if not mine:
            return
        boss = mine[0]
    aide = aide_of(boss)
    others = [c for c in T.cores if c != boss]
    X = [c for c in others if topo.same_plane(boss, c)][0]
    D = [c for c in others if not topo.may_write(boss, c)][0]
    Y = [c for c in others if c != X and c != D][0]
    kap = [T.rank_of(D), T.rank_of(Y), T.rank_of(X), T.rank_of(boss)]
    ex_mask = topo.mask(boss, aide) & topo.mask(boss, X)

    def bits(m):
        return bin(m).count("1")

    def engines(src, dst):
        return bits(topo.mask(src, dst))

    tot = {}

    def inc(ins, name, n=1):
        ins.then_inc(T.sem[name], n)
        tot[name] = tot.get(name, 0) + n
        return tot[name]

    def onehot(buf, k):
        return inc(V.tensor_scalar(buf[:, k:8:4], T.exn[:, 0:9:8], float(kap[k]), None, A.is_equal), "v")

    def send(dst, out_ap, in_ap, sem, mask=None):
        rid, pid = topo.addr(dst, core)
        m = topo.mask(core, dst) if mask is None else mask
        g.remote_dma(out_ap, in_ap, T.sem[sem], T.sem.ls, pid, rid, m)
        tot["ls"] = tot.get("ls", 0) + bits(m)

    def finish():
        for name in SEMAPHORES:
            if tot.get(name, 0):
                g.wait_ge(T.sem[name], tot[name])

    if core != boss:
        inc(g.iota(T.i1[:, :], [[1, 128]], 0, -1), "gi")
        inc(g.iota(T.k2[:, :], [[-16, 8]], 0, 1), "gi")
        inc(V.memset(T.ones[:, :], 1.0), "v")
        V.wait_ge(T.sem.gi, tot["gi"])
        inc(V.tensor_scalar(T.lt[:, :], T.i1[:, :], 0, None, A.is_gt), "v")
        inc(V.tensor_scalar(T.k3[:, :], T.k2[:, :], 4, None, A.arith_shift_right), "v")
        inc(V.tensor_scalar(T.ri2[:, :], T.i1[:, :], 15, None, A.bitwise_and), "v")
        V.wait_ge(T.sem.v, tot["v"])
        inc(V.tensor_scalar(T.bm[:, :], T.k3[:, :], 0, None, A.is_equal), "v")
        inc(V.tensor_scalar(T.r1[:, :], T.ri2[:, :], 0, None, A.is_equal), "v")
        tot["aE"] = bits(ex_mask)
        V.wait_ge(T.sem.aE, tot["aE"])
        for k in range(4):
            onehot(T.m8, k)
        for k in range(4):
            onehot(T.mf, k)
        P.wait_ge(T.sem.v, tot["v"])
        inc(P.matmul(T.yp2[:, 0:4], T.lt[:, :], T.m8[:, 0:4], True, True), "pc1")
        inc(P.matmul(T.yp2[:, 4:8], T.lt[:, :], T.m8[:, 4:8], True, False), "pc1")
        inc(P.matmul(T.yp2[:, 4:8], T.ones[:, :], T.m8[:, 0:4], False, True), "pc1")
        V.wait_ge(T.sem.pc1, tot["pc1"])
        for k in range(4):
            inc(V.tensor_scalar(T.cs[:, k:8:4], T.yp2[:, k:8:4], float(CAP), float(PITCH * k - MID), A.min, A.add), "v")
        V.wait_ge(T.sem.v, tot["v"])
        for k in range(4):
            for h in range(2):
                i = 4 * h + k
                inc(V.tensor_scalar(T.rk[:, 16 * k + 8 * h:16 * k + 8 * h + 8], T.bm[:, :], T.cs[:, i:i + 1],
                                    T.mf[:, i:i + 1], A.mult, A.mult), "v")
        P.wait_ge(T.sem.v, tot["v"])
        for k in range(4):
            inc(P.matmul(T.yp3[:, 0:16], T.r1[:, :], T.rk[:, 16 * k:16 * k + 16], k == 0, k == 3), "pi3")
        V.wait_ge(T.sem.pi3, tot["pi3"])
        inc(V.tensor_scalar(T.off2[:, :], T.yp3[:, 0:16], float(MID), None, A.add), "v")
        g.wait_ge(T.sem.v, tot["v"])
        send(boss, T.off2[:, :], T.off2[:, :], "aO")
        finish()
        return

    for a in range(8):
        inc((Q if a < 4 else S).dma_start(T.exn[16 * a:16 * a + 16, :], T.ex[:, a:a + 9]), "sex", 16)
    inc(Q.dma_start(T.xs[0:64, :], T.x[0:64, :]), "sx", 16)
    inc(S.dma_start(T.xs[64:128, :], T.x[64:128, :]), "sx", 16)
    inc(Q.dma_start(T.w1s[:, :], T.w1[:, :]), "sw1", 16)
    inc(S.dma_start(T.w2s[:, :], T.w2[:, :]), "sw2", 16)

    inc(g.iota(T.i1[:, :], [[1, 128]], 0, -1), "gi")
    g_j = inc(g.iota(T.jj[:, :], [[1, 80]], 0, 0), "gq")
    inc(V.memset(T.ones[:, :], 1.0), "v")
    V.wait_ge(T.sem.gi, tot["gi"])
    inc(V.tensor_scalar(T.lt[:, :], T.i1[:, :], 0, None, A.is_gt), "v")
    inc(V.tensor_scalar(T.idn[:, :], T.i1[:, :], 0, None, A.is_equal), "v")

    g.wait_ge(T.sem.sex, tot["sex"])
    send(aide, T.exn[:, :], T.exn[:, :], "aE", ex_mask)

    V.wait_ge(T.sem.sex, tot["sex"])
    v_md = onehot(T.m8, 0)
    v_fd = onehot(T.mf, 0)
    for k in range(1, 4):
        v_mr = onehot(T.m8, k)
    for k in range(1, 4):
        v_fr = onehot(T.mf, k)
    P.wait_ge(T.sem.v, v_md)
    inc(P.matmul(T.yp2[:, 0:1], T.lt[:, :], T.m8[:, 0:1], True, True), "pc1")
    inc(P.matmul(T.yp2[:, 1:2], T.lt[:, :], T.m8[:, 4:5], True, False), "pc1")
    inc(P.matmul(T.yp2[:, 1:2], T.ones[:, :], T.m8[:, 0:1], False, True), "pc1")
    P.wait_ge(T.sem.sx, tot["sx"])
    inc(P.matmul(T.hp0[:, 0:128], T.xs[:, 0:128], T.idn[:, :], True, True), "pt")
    inc(P.matmul(T.hp1[:, 0:128], T.xs[:, 128:256], T.idn[:, :], True, True), "pt")
    P.wait_ge(T.sem.v, v_mr)
    inc(P.matmul(T.yp3[:, 0:3], T.lt[:, :], T.m8[:, 1:4], True, True), "pc2")
    inc(P.matmul(T.yp3[:, 3:6], T.lt[:, :], T.m8[:, 5:8], True, False), "pc2")
    inc(P.matmul(T.yp3[:, 3:6], T.ones[:, :], T.m8[:, 1:4], False, True), "pc2")
    for h, bank in enumerate((T.hp0, T.hp1)):
        S.wait_ge(T.sem.pt, h + 1)
        s_xt = inc(S.activation(T.xt[:, 128 * h:128 * h + 128], bank[:, 0:128], F.Copy), "sc")

    def place(k, h):
        return T.yp2[:, h:h + 1] if k == 0 else T.yp3[:, 3 * h + k - 1:3 * h + k]

    v_sel = []
    V.wait_ge(T.sem.gq, g_j)
    for k in range(4):
        if k < 2:
            V.wait_ge(T.sem.v, v_fd if k == 0 else v_fr)
            V.wait_ge(T.sem["pc1" if k == 0 else "pc2"], 3)
        for h in range(2):
            c = 160 * k + 80 * h
            n = inc(V.tensor_scalar(T.sel[:, c:c + 80], T.jj[:, :], place(k, h), T.mf[:, 4 * h + k:4 * h + k + 1],
                                    A.is_equal, A.mult), "v")
        v_sel.append(n)
    dps = [T.hp2, T.hp3, T.yp1, T.yp0]
    s_cp = []
    P.wait_ge(T.sem.sc, s_xt)
    for k in range(4):
        P.wait_ge(T.sem.v, v_sel[k])
        for h in range(2):
            c = 160 * k + 80 * h
            n = inc(P.matmul(dps[k][:, 0:CAP], T.xt[:, 128 * h:128 * h + 128], T.sel[:, c:c + 80], h == 0, h == 1), "pd")
        S.wait_ge(T.sem.pd, n)
        s_cp.append(inc(S.activation(T.xb[:, CAP * k:CAP * k + CAP], dps[k][:, 0:CAP], F.Copy), "sc"))

    for k in range(4):
        inc(V.memset(T.res[:, PITCH * k + CAP:PITCH * k + PITCH], 0.0), "v")

    for name, src in (("aP", X), ("aX", X), ("aY", Y), ("aD", Y), ("rP", X), ("rX", X), ("rY", Y), ("rD", Y), ("aO", aide)):
        tot[name] = engines(src, core)

    g.wait_ge(T.sem.sc, s_cp[0])
    send(X, T.xin[:, 80:160], T.xb[:, 0:80], "aP")
    g.wait_ge(T.sem.sc, s_cp[1])
    send(Y, T.xin[:, 160:240], T.xb[:, 80:160], "aY")
    g.wait_ge(T.sem.sc, s_cp[2])
    send(X, T.xin[:, 0:80], T.xb[:, 160:240], "aX")
    g.wait_ge(T.sem.aP, tot["aP"])
    send(Y, T.xin[:, 240:320], T.xin[:, 80:160], "aD")

    hp = [T.hp0, T.hp1, T.hp2, T.hp3]
    yp = [T.yp0, T.yp1, T.yp2, T.yp3]
    blocks = [(T.xb[:, 240:320], None, T.res[:, 3 * PITCH:3 * PITCH + CAP]),
              (T.xin[:, 160:240], "aY", T.outb[:, 80:160]),
              (T.xin[:, 240:320], "aD", T.outb[:, 0:80]),
              (T.xin[:, 0:80], "aX", T.outb[:, 160:240])]
    P.wait_ge(T.sem.sc, s_cp[3])
    P.wait_ge(T.sem.sw1, tot["sw1"])
    for b, (rhs, arr, dest) in enumerate(blocks):
        if arr:
            P.wait_ge(T.sem[arr], tot[arr])
        for i in range(4):
            if b:
                P.wait_ge(T.sem["rh%d" % i], b)
            for f in (2 * i, 2 * i + 1):
                c = (f % 2) * CAP
                inc(P.matmul(hp[i][:, c:c + CAP], T.w1s[:, 128 * f:128 * f + 128], rhs, True, True), "mh%d" % i)
        for i in range(4):
            h = T.hs[:, b * 640 + i * 160:b * 640 + i * 160 + 160]
            E = V if i % 2 == 0 else S
            E.wait_ge(T.sem["mh%d" % i], tot["mh%d" % i])
            if i % 2 == 0:
                inc(V.tensor_scalar(h, hp[i][:, 0:160], 0.0, None, A.max), "rh%d" % i)
            else:
                inc(S.activation(h, hp[i][:, 0:160], F.Relu), "rh%d" % i)
        if b == 0:
            P.wait_ge(T.sem.sw2, tot["sw2"])
        for i in range(4):
            P.wait_ge(T.sem["rh%d" % i], b + 1)
            for f in (2 * i, 2 * i + 1):
                c = b * 640 + f * CAP
                inc(P.matmul(yp[b][:, 0:CAP], T.w2s[:, 128 * f:128 * f + 128], T.hs[:, c:c + CAP], f == 0, f == 7),
                    "my%d" % b)
        V.wait_ge(T.sem["my%d" % b], tot["my%d" % b])
        inc(V.tensor_copy(dest, yp[b][:, 0:CAP]), "yc%d" % b)

    g.wait_ge(T.sem.yc1, tot["yc1"])
    send(Y, T.res[:, PITCH:PITCH + CAP], T.outb[:, 80:160], "rY")
    g.wait_ge(T.sem.yc2, tot["yc2"])
    send(X, T.stg[:, :], T.outb[:, 0:80], "rP")
    g.wait_ge(T.sem.yc3, tot["yc3"])
    send(X, T.res[:, 2 * PITCH:2 * PITCH + CAP], T.outb[:, 160:240], "rX")
    g.wait_ge(T.sem.rP, tot["rP"])
    send(Y, T.res[:, 0:CAP], T.stg[:, :], "rD")

    for E in (V, S):
        for name in ("v", "yc0", "aO", "rX", "rY", "rD"):
            E.wait_ge(T.sem[name], tot[name])
    inc(V.tensor_copy(T.ys[:, 0:128], T.res[:, 0:4 * PITCH].indirect(T.off2[:, 0:8])), "gv")
    inc(S.activation(T.ys[:, 128:256], T.res[:, 0:4 * PITCH].indirect(T.off2[:, 8:16]), F.Copy), "ga")
    Q.wait_ge(T.sem.gv, tot["gv"])
    Q.wait_ge(T.sem.ga, tot["ga"])
    inc(Q.dma_start(T.y[:, :], T.ys[:, :]), "sy", 16)
    finish()
